import numpy as np
import ml_dtypes


def mxq(x, axis, fmt="e4m3"):
    dtype, down = {"e4m3": (ml_dtypes.float8_e4m3fn, 7), "e5m2": (ml_dtypes.float8_e5m2, 14)}[fmt]
    v = np.moveaxis(np.asarray(x, np.float32).astype(ml_dtypes.bfloat16).astype(np.float64), axis, -1)
    blocks = v.reshape(v.shape[:-1] + (-1, 32))
    amax = np.abs(blocks).max(-1, keepdims=True)
    byte = np.maximum(np.where(amax > 0, np.frexp(amax)[1] - 1 + 127, 0) - down, 1)
    scale = np.exp2(byte - 127.0)
    codes = (blocks / scale).astype(np.float32).astype(dtype).astype(np.float64)
    return np.moveaxis((codes * scale).reshape(v.shape), -1, axis)


WIDE = False


def mx_kscale(k):
    if not WIDE:
        return np.ones(k)
    levels = np.array([10, -10, 5, -5, 0])
    if k % 512:
        return np.exp2(np.random.permutation(np.resize(levels, k // 32))).repeat(32)
    a = np.empty((k // 512, 16))
    for p in range(k // 512):
        a[p, :8] = np.random.permutation(np.resize(levels, 8))
        for g in range(8):
            far = levels[np.abs(levels - a[p, g]) >= 10]
            a[p, g + 8] = far[np.random.randint(len(far))]
    return np.exp2(a.ravel()).repeat(32)


def f64(x):
    return np.asarray(x).astype(np.float64)


def striped(idx):
    return np.tile(np.asarray(idx).reshape(-1, 16).T, (8, 1)).astype(np.uint16)


def unstriped(offs):
    return offs[:16].T.reshape(-1).astype(np.int64)


E2M1 = np.array([0.0, 0.5, 1.0, 1.5, 2.0, 3.0, 4.0, 6.0, -0.0, -0.5, -1.0, -1.5, -2.0, -3.0, -4.0, -6.0])


def pack_weight(w, fmt):
    k, n = w.shape
    w = f64(np.asarray(w, np.float32).astype(ml_dtypes.bfloat16)).reshape(k // 32, 32, n)
    amax = np.abs(w).max(1)
    if fmt == "e4m3":
        byte = np.frexp(amax)[1] - 1 + 127 - 7
    else:
        mant, ex = np.frexp(amax / 6.0)
        byte = np.where(mant > 0.5, ex, ex - 1) + 127
    byte = np.clip(np.where(amax > 0, byte, 1), 1, 254)
    scaled = (w * np.exp2(127.0 - byte)[:, None, :]).reshape(k, n).astype(np.float32)
    by_word = np.ascontiguousarray(scaled.reshape(k // 512, 128, 4, n).transpose(0, 1, 3, 2))
    if fmt == "e4m3":
        words = by_word.astype(ml_dtypes.float8_e4m3fn).view(np.uint8)
    else:
        c = by_word.astype(ml_dtypes.float4_e2m1fn).view(np.uint8) & 0xF
        words = (c[..., 0::2] | (c[..., 1::2] << 4)).reshape(k // 512, 128, 2 * n)
    return np.ascontiguousarray(words), np.ascontiguousarray(byte.astype(np.uint8).reshape(k // 512, 16, n))


def unpack_weight(words, scales, fmt):
    g, _, n = scales.shape
    words = np.ascontiguousarray(words).reshape(g, 128, n, -1)
    if fmt == "e4m3":
        vals = words.view(ml_dtypes.float8_e4m3fn).astype(np.float64)
    else:
        nib = np.empty((g, 128, n, 4), np.uint8)
        nib[..., 0::2] = words & 0xF
        nib[..., 1::2] = words >> 4
        vals = E2M1[nib]
    vals = vals * np.repeat(np.exp2(scales.astype(np.float64) - 127.0), 8, axis=1)[..., None]
    return vals.transpose(0, 1, 3, 2).reshape(g * 512, n)


D, T, I, J, U, E, N = 512, 2048, 512, 512, 1024, 512, 64


def setup_inputs():
    n = np.random.standard_normal
    idx = np.random.permutation(T)[:I]
    idx2 = np.random.permutation(U)[:J]
    idx3 = np.random.permutation(U)[:J]
    fd = mx_kscale(D)
    fi = mx_kscale(I)
    ti = np.ones(T)
    ti[idx] = fi
    keysp = pack_weight(n((D, T)) / fd[:, None], "e4m3")
    return {
        "keys_words": keysp[0],
        "keys_scales": keysp[1],
        "notes": (n((D, U)) * 1.0 / np.sqrt(D) * fd[:, None]).astype(np.float32),
        "rowf": (np.random.uniform(0.02, 0.08, (I, 1)) * fi[:, None]).astype(np.float32),
        "vals": (n((E, T)) / ti).astype(np.float32),
        "offs": striped(idx),
        "offs2": striped(idx2),
        "offs3": striped(idx3),
    }


def reference(keys_words, keys_scales, notes, rowf, vals, offs, offs2, offs3):
    idx = unstriped(offs)
    idx2 = unstriped(offs2)
    idx3 = unstriped(offs3)
    keysu = unpack_weight(keys_words, keys_scales, "e4m3")
    keysidxg = keysu[:, idx]
    notesq = mxq(f64(notes), 0, "e4m3")
    g1 = keysidxg.T @ notesq
    g0 = g1[:, idx2] - g1[:, idx3]
    gr1 = g0 * f64(rowf)
    vt1 = f64(vals)[:, idx].T
    vt1q = mxq(vt1, 0, "e4m3")
    gr1q = mxq(gr1, 0, "e4m3")
    o = vt1q.T @ gr1q
    y = o.reshape(E, N, J // N).max(axis=2)
    return y

from contextlib import ExitStack

import concourse.mybir as mybir
from concourse.masks import make_identity

D, T, I, J, U, E, N = 512, 2048, 512, 512, 1024, 512, 64
FLOPS = 2 * D * I * U + 2 * I * E * J

F32 = mybir.dt.float32
BF16 = mybir.dt.bfloat16
I32 = mybir.dt.int32
U32 = mybir.dt.uint32
U16 = mybir.dt.uint16
U8 = mybir.dt.uint8
FP8X4 = mybir.dt.float8_e4m3fn_x4
COPY = mybir.ActivationFunctionType.Copy
ALU = mybir.AluOpType

P = 128
PACK = 4
RUN = J // N
NOTE_COLS = 256
J_COLS = 256


def tile_attend_tab_looked_bestruns_kernel(tc, keys_words, keys_scales, notes, rowf, vals, offs, offs2, offs3, out):
    nc = tc.nc
    with ExitStack() as ctx:
        lists = ctx.enter_context(tc.tile_pool(name="lists", bufs=1))
        sb = ctx.enter_context(tc.tile_pool(name="sb", bufs=1))
        psum = ctx.enter_context(tc.psum_pool(name="psum", bufs=1))

        idx = lists.tile([P, I // 16], U16, name="idx")
        idx2 = lists.tile([P, J // 16], U16, name="idx2")
        idx3 = lists.tile([P, J // 16], U16, name="idx3")

        pool_scales = sb.tile([P, T], U8, name="pool_scales", align_bytes=64)
        nc.gpsimd.memset(pool_scales[:].bitcast(I32), 0)
        notes_view = notes.rearrange("(p t) u -> p t u", t=PACK)
        chunks = U // NOTE_COLS
        notes_raw = [sb.tile([P, PACK, NOTE_COLS], F32, name=f"notes_raw{c}", align_bytes=64) for c in range(chunks)]

        def load_notes(c):
            nc.sync.dma_start(notes_raw[c][:], notes_view[:, :, c * NOTE_COLS : (c + 1) * NOTE_COLS])

        nc.sync.dma_start(idx[:], offs)
        load_notes(0)
        for q in range(4):
            nc.sync.dma_start(
                pool_scales[32 * q : 32 * q + 4, :].bitcast(I32), keys_scales[0, 4 * q : 4 * q + 4, :].bitcast(I32)
            )
        pool_words = sb.tile([P, T], U32, name="pool_words", align_bytes=64)
        nc.sync.dma_start(pool_words[:].bitcast(I32), keys_words[0].rearrange("p n t -> p (n t)").bitcast(I32))
        for c in range(1, chunks):
            load_notes(c)
        nc.sync.dma_start(idx3[:], offs3)
        nc.sync.dma_start(idx2[:], offs2)
        factor = sb.tile([P, PACK], F32, name="factor")
        nc.sync.dma_start(factor[:], rowf.rearrange("(p r) o -> p (r o)", r=PACK))
        vals_view = vals.rearrange("(p b) t -> b p t", b=PACK)
        vals_pool = []
        for b in range(PACK):
            v = sb.tile([P, T], F32, name=f"vals_pool{b}", tag=f"slot{b}", align_bytes=64)
            nc.sync.dma_start(v[:], vals_view[b])
            vals_pool.append(v)

        ident = sb.tile([P, P], F32, name="ident", align_bytes=64)
        make_identity(nc, ident[:])

        key_scales = sb.tile([P, I], U8, name="key_scales", align_bytes=64)
        nc.vector.tensor_copy(key_scales[:].rearrange("p (r s) -> p s r", r=PACK), pool_scales[:].indirect(idx[:]))
        key_words = sb.tile([P, I], U32, name="key_words", align_bytes=64)
        nc.vector.tensor_copy(key_words[:].rearrange("p (r s) -> p s r", r=PACK), pool_words[:].indirect(idx[:]))

        g1 = [sb.tile([P, U], F32, name=f"g1_{r}", align_bytes=64) for r in range(PACK)]
        for c in range(chunks):
            grouped = sb.tile([P, NOTE_COLS, PACK], BF16, name=f"notes_bf{c}", align_bytes=64)
            dst = grouped[:].rearrange("p (c i) t -> p c t i", i=4)
            src = notes_raw[c][:].rearrange("p t (c i) -> p c t i", i=4)
            nc.vector.tensor_copy(dst, src)
            codes = sb.tile([P, NOTE_COLS], U32, name=f"notes_codes{c}", align_bytes=64)
            scales = sb.tile([P, NOTE_COLS], U8, name=f"notes_scales{c}", align_bytes=64)
            nc.vector.quantize_mx(out=codes[:].bitcast(FP8X4), scales=scales[:], in_=grouped[:].rearrange("p w t -> p (w t)"))
            for r in range(PACK):
                acc = psum.tile([P, NOTE_COLS], F32, name="acc", tag="acc", bufs=6)
                cols = slice(r * P, (r + 1) * P)
                nc.tensor.matmul_mx(
                    out=acc[:], lhsT=key_words[:, cols].bitcast(FP8X4), lhsT_scale=key_scales[:, cols],
                    rhs=codes[:].bitcast(FP8X4), rhs_scale=scales[:], start=True, stop=True,
                )
                dst = g1[r][:, c * NOTE_COLS : (c + 1) * NOTE_COLS]
                if c == chunks - 1 and r > 0:
                    nc.vector.tensor_copy(dst, acc[:])
                else:
                    nc.scalar.copy(dst, acc[:])

        table_codes = sb.tile([P, J], U32, name="table_codes", align_bytes=64)
        table_scales = sb.tile([P, J], U8, name="table_scales", align_bytes=64)
        for h in range(J // J_COLS):
            entries = slice(h * J_COLS // 16, (h + 1) * J_COLS // 16)
            diff = sb.tile([P, PACK, J_COLS], F32, name=f"diff{h}", align_bytes=64)
            for r in range(PACK):
                minus = sb.tile([P, J_COLS], F32, name=f"minus{h}_{r}", align_bytes=64)
                nc.scalar.activation(minus[:], g1[r][:].indirect(idx3[:, entries]), COPY)
                nc.vector.tensor_tensor(diff[:, r, :], g1[r][:].indirect(idx2[:, entries]), minus[:], ALU.subtract)
            grouped = sb.tile([P, J_COLS, PACK], BF16, name=f"table_bf{h}", align_bytes=64)
            nc.vector.tensor_tensor(
                grouped[:].rearrange("p (c i) r -> p c r i", i=4),
                diff[:].rearrange("p r (c i) -> p c r i", i=4),
                factor[:].unsqueeze(1).unsqueeze(3).broadcast_to([P, J_COLS // 4, PACK, 4]),
                ALU.mult,
            )
            cols = slice(h * J_COLS, (h + 1) * J_COLS)
            nc.vector.quantize_mx(
                out=table_codes[:, cols].bitcast(FP8X4), scales=table_scales[:, cols],
                in_=grouped[:].rearrange("p w r -> p (w r)"),
            )

        out_view = out.rearrange("(p b) n -> b p n", b=PACK)
        turned, sums = {}, {}

        def pick(b):
            picked = sb.tile([P, I], BF16, name=f"picked{b}", align_bytes=64)
            nc.scalar.activation(picked[:], vals_pool[b][:].indirect(idx[:]), COPY)
            words = picked[:].bitcast(F32)
            turned[b] = psum.tile([P, 2, P], F32, name="turned", tag="turned", bufs=2)
            for u in range(2):
                nc.tensor.transpose(turned[b][:, u, :], words[:, u : I // 2 : 2], ident[:])

        def multiply(b):
            grouped = sb.tile([P, P * PACK], BF16, name=f"vals_bf{b}", tag=f"slot{b + 1}", align_bytes=64)
            nc.scalar.copy(grouped[:].bitcast(F32).rearrange("p (e u) -> p e u", u=2), turned[b][:].rearrange("p u e -> p e u"))
            codes = sb.tile([P, P], U32, name=f"vals_codes{b}", align_bytes=64)
            scales = sb.tile([P, P], U8, name=f"vals_scales{b}", align_bytes=64)
            nc.vector.quantize_mx(out=codes[:].bitcast(FP8X4), scales=scales[:], in_=grouped[:])
            sums[b] = psum.tile([P, J], F32, name="acc", tag="acc", bufs=6)
            nc.tensor.matmul_mx(
                out=sums[b][:], lhsT=codes[:].bitcast(FP8X4), lhsT_scale=scales[:],
                rhs=table_codes[:].bitcast(FP8X4), rhs_scale=table_scales[:], start=True, stop=True,
            )

        def best_of_runs(b):
            best = sb.tile([P, N], F32, name=f"best{b}", tag=f"slot{b + 2}", align_bytes=64)
            nc.vector.tensor_reduce(best[:], sums[b][:].rearrange("p (n k) -> p n k", k=RUN), mybir.AxisListType.X, ALU.max)
            nc.sync.dma_start(out_view[b], best[:])

        for step in range(PACK + 2):
            if step < PACK:
                pick(step)
            if 1 <= step <= PACK:
                multiply(step - 1)
            if step >= 2:
                best_of_runs(step - 2)
